import numpy as np
import ml_dtypes


def mxq(x, axis, fmt="e4m3"):
    dtype, down = {"e4m3": (ml_dtypes.float8_e4m3fn, 7), "e5m2": (ml_dtypes.float8_e5m2, 14)}[fmt]
    v = np.moveaxis(np.asarray(x, np.float32).astype(ml_dtypes.bfloat16).astype(np.float64), axis, -1)
    blocks = v.reshape(v.shape[:-1] + (-1, 32))
    amax = np.abs(blocks).max(-1, keepdims=True)
    byte = np.maximum(np.where(amax > 0, np.frexp(amax)[1] - 1 + 127, 0) - down, 1)
    scale = np.exp2(byte - 127.0)
    codes = (blocks / scale).astype(np.float32).astype(dtype).astype(np.float64)
    return np.moveaxis((codes * scale).reshape(v.shape), -1, axis)


WIDE = False


def mx_kscale(k):
    if not WIDE:
        return np.ones(k)
    levels = np.array([10, -10, 5, -5, 0])
    if k % 512:
        return np.exp2(np.random.permutation(np.resize(levels, k // 32))).repeat(32)
    a = np.empty((k // 512, 16))
    for p in range(k // 512):
        a[p, :8] = np.random.permutation(np.resize(levels, 8))
        for g in range(8):
            far = levels[np.abs(levels - a[p, g]) >= 10]
            a[p, g + 8] = far[np.random.randint(len(far))]
    return np.exp2(a.ravel()).repeat(32)


def f64(x):
    return np.asarray(x).astype(np.float64)


def striped(idx):
    return np.tile(idx.reshape(-1, 16).T, (8, 1)).astype(np.uint16)


def unstriped(offs):
    return offs[:16].T.reshape(-1).astype(np.int64)


E2M1 = np.array([0.0, 0.5, 1.0, 1.5, 2.0, 3.0, 4.0, 6.0, -0.0, -0.5, -1.0, -1.5, -2.0, -3.0, -4.0, -6.0])


def pack_weight(w, fmt):
    k, n = w.shape
    w = f64(np.asarray(w, np.float32).astype(ml_dtypes.bfloat16)).reshape(k // 32, 32, n)
    amax = np.abs(w).max(1)
    if fmt == "e4m3":
        byte = np.frexp(amax)[1] - 1 + 127 - 7
    else:
        mant, ex = np.frexp(amax / 6.0)
        byte = np.where(mant > 0.5, ex, ex - 1) + 127
    byte = np.clip(np.where(amax > 0, byte, 1), 1, 254)
    scaled = (w * np.exp2(127.0 - byte)[:, None, :]).reshape(k, n).astype(np.float32)
    by_word = np.ascontiguousarray(scaled.reshape(k // 512, 128, 4, n).transpose(0, 1, 3, 2))
    if fmt == "e4m3":
        words = by_word.astype(ml_dtypes.float8_e4m3fn).view(np.uint8)
    else:
        c = by_word.astype(ml_dtypes.float4_e2m1fn).view(np.uint8) & 0xF
        words = (c[..., 0::2] | (c[..., 1::2] << 4)).reshape(k // 512, 128, 2 * n)
    return np.ascontiguousarray(words), np.ascontiguousarray(byte.astype(np.uint8).reshape(k // 512, 16, n))


def unpack_weight(words, scales, fmt):
    g, _, n = scales.shape
    words = np.ascontiguousarray(words).reshape(g, 128, n, -1)
    if fmt == "e4m3":
        vals = words.view(ml_dtypes.float8_e4m3fn).astype(np.float64)
    else:
        nib = np.empty((g, 128, n, 4), np.uint8)
        nib[..., 0::2] = words & 0xF
        nib[..., 1::2] = words >> 4
        vals = E2M1[nib]
    vals = vals * np.repeat(np.exp2(scales.astype(np.float64) - 127.0), 8, axis=1)[..., None]
    return vals.transpose(0, 1, 3, 2).reshape(g * 512, n)


def gelu(v):
    return 0.5 * v * (1.0 + np.tanh(np.sqrt(2.0 / np.pi) * (v + 0.044715 * v**3)))


K, H, T, S, T3, S2, P = 1536, 512, 4096, 1024, 2048, 1024, 512

def setup_inputs():
    n = np.random.standard_normal
    s = mx_kscale(K)[:, None]
    u = mx_kscale(H)[:, None]
    d = {}
    d["tab_words"], d["tab_scales"] = pack_weight(n((K, T)) * s, "e4m3")
    d["offs"] = striped(np.random.permutation(T)[:S])
    d["tab2_words"], d["tab2_scales"] = pack_weight(n((H, T3)) / H ** 0.5 / u, "e4m3")
    d["offs2"] = striped(np.random.permutation(T3)[:S2])
    d["pos1"] = striped(np.random.permutation(S)[:P])
    d["pos2"] = striped(np.random.permutation(S)[:P])
    d["w1"] = (1.5 * n((K, H)) / K ** 0.5 / s).astype(np.float32)
    d["b1"] = (0.6 * n(H)).astype(np.float32)
    d["w4_words"], d["w4_scales"] = pack_weight(n((K, H)) / K ** 0.5 / s, "e2m1")
    d["gain"] = (np.exp(0.3 * n(H)) * u[:, 0]).astype(np.float32)
    d["base"] = (0.8 * n(S2)).astype(np.float32)
    return d

def reference(tab_words, tab_scales, offs, tab2_words, tab2_scales, offs2, pos1, pos2,
              w1, b1, w4_words, w4_scales, gain, base):
    v = unpack_weight(tab_words, tab_scales, "e4m3")[:, unstriped(offs)]
    v2 = unpack_weight(tab2_words, tab2_scales, "e4m3")[:, unstriped(offs2)]
    w4 = unpack_weight(w4_words, w4_scales, "e2m1")
    tread = np.tanh((mxq(f64(w1), 0, "e4m3").T @ v) + f64(b1)[:, None])
    wear = w4.T @ v
    h = np.maximum(tread, wear) * f64(gain)[:, None]
    e = v2.T @ mxq(h, 0, "e4m3")
    diff = e[:, unstriped(pos1)] - e[:, unstriped(pos2)]
    return np.maximum(diff, f64(base)[:, None])

@@ -1,0 +1,269 @@
+from contextlib import ExitStack
+
+import concourse.mybir as mybir
+
+K, H, T, S, T2, S2, PAIRS = 1536, 512, 4096, 1024, 2048, 1024, 512
+FLOPS = 2 * K * H * S * 2 + 2 * H * S2 * S
+
+F32 = mybir.dt.float32
+BF16 = mybir.dt.bfloat16
+I32 = mybir.dt.int32
+U32 = mybir.dt.uint32
+U16 = mybir.dt.uint16
+U8 = mybir.dt.uint8
+FP8X4 = mybir.dt.float8_e4m3fn_x4
+FP4X4 = mybir.dt.float4_e2m1fn_x4
+ACT = mybir.ActivationFunctionType
+ALU = mybir.AluOpType
+
+P = 128
+PACK = 4
+PASSES = K // (P * PACK)
+N = 512
+HALVES = S // N
+QUADS = 4
+M_TILES = S2 // P
+
+
+def tile_list_sole_link_scores_kernel(
+    tc, tab_words, tab_scales, offs, tab2_words, tab2_scales, offs2, pos1, pos2,
+    w1, b1, w4_words, w4_scales, gain, base, out,
+):
+    nc = tc.nc
+    with ExitStack() as ctx:
+        keep = ctx.enter_context(tc.tile_pool(name="keep", bufs=1))
+        ring = ctx.enter_context(tc.tile_pool(name="ring", bufs=4))
+        stream = ctx.enter_context(tc.tile_pool(name="stream", bufs=3))
+        psum = ctx.enter_context(tc.psum_pool(name="psum", bufs=1))
+
+        def held(shape, dtype, name):
+            return keep.tile(shape, dtype, name=name, align_bytes=64)
+
+        def bank(b):
+            return psum.tile([P, N], F32, name="bank%d" % b)
+
+        offs_sb = held([P, S // 16], U16, "offs_sb")
+        offs2_sb = held([P, S2 // 16], U16, "offs2_sb")
+        pos1_sb = held([P, PAIRS // 16], U16, "pos1_sb")
+        pos2_sb = held([P, PAIRS // 16], U16, "pos2_sb")
+
+        def streamed(shape, dtype):
+            return stream.tile(shape, dtype, name="streamed", align_bytes=64)
+
+        tab_s = held([P, T], U8, "tab_s")
+        tab2_s = held([P, T2], U8, "tab2_s")
+        w4s_raw = held([P, PASSES, H], U8, "w4s_raw")
+        v_s = [held([P, S], U8, "v_s%d" % a) for a in range(PASSES)]
+        warm = held([P, 1], F32, "warm")
+        warm_out = held([P, 1], F32, "warm_out")
+        b1_sb = held([P, PACK], F32, "b1_sb")
+        gain_sb = held([P, PACK], F32, "gain_sb")
+
+        nc.vector.memset(tab_s[:].bitcast(I32), 0)
+        nc.vector.memset(w4s_raw[:].rearrange("p a c -> p (a c)").bitcast(I32), 0)
+        nc.vector.memset(tab2_s[:].bitcast(I32), 0)
+        for a in range(1, PASSES):
+            nc.vector.memset(v_s[a][:].bitcast(I32), 0)
+        nc.vector.memset(warm[:], 0.0)
+
+        def load_table(a):
+            words = streamed([P, T], I32)
+            nc.sync.dma_start(words[:], tab_words[a].rearrange("p t i -> p (t i)").bitcast(I32))
+            return words
+
+        nc.sync.dma_start(offs_sb[:], offs)
+        nc.sync.dma_start(offs2_sb[:], offs2)
+        nc.sync.dma_start(b1_sb[:], b1.rearrange("(p t) -> p t", t=PACK))
+        nc.sync.dma_start(gain_sb[:], gain.rearrange("(p t) -> p t", t=PACK))
+        w4_raw = streamed([P, PASSES, 2 * H], U8)
+        nc.sync.dma_start(w4_raw[:].bitcast(I32), w4_words.rearrange("a p c -> p a c").bitcast(I32))
+        tab_w = [load_table(0), load_table(1)]
+        nc.sync.dma_start(pos1_sb[:], pos1)
+        nc.sync.dma_start(pos2_sb[:], pos2)
+        for q in range(QUADS):
+            nc.gpsimd.dma_start(
+                tab_s[32 * q : 32 * q + 4 * PASSES, :].bitcast(I32),
+                tab_scales[:, 4 * q : 4 * q + 4, :].bitcast(I32),
+            )
+        for q in range(QUADS):
+            nc.scalar.dma_start(
+                w4s_raw[32 * q : 32 * q + 4, :, :].bitcast(I32),
+                w4_scales[:, 4 * q : 4 * q + 4, :].rearrange("a r c -> r a c").bitcast(I32),
+            )
+        for q in range(QUADS):
+            nc.gpsimd.dma_start(
+                tab2_s[32 * q : 32 * q + 4, :].bitcast(I32),
+                tab2_scales[0, 4 * q : 4 * q + 4, :].bitcast(I32),
+            )
+        nc.scalar.activation(warm_out[:], warm[:], ACT.Tanh)
+
+        w4_w = held([P, PASSES, 2 * H], U8, "w4_w")
+        w4_s = held([P, PASSES, H], U8, "w4_s")
+        nc.vector.tensor_copy(
+            w4_w[:].bitcast(U16).rearrange("p a (t m) -> p a m t", t=PACK),
+            w4_raw[:].bitcast(U16).rearrange("p a (m t) -> p a m t", t=PACK),
+        )
+        nc.vector.tensor_copy(
+            w4_s[:].rearrange("p a (t m) -> p a m t", t=PACK),
+            w4s_raw[:].rearrange("p a (m t) -> p a m t", t=PACK),
+        )
+
+        tab_w.append(load_table(2))
+        v_w = {}
+        wear_ps = {}
+        order = list(reversed(range(HALVES)))
+        for h in order:
+            for t in range(PACK):
+                wear_ps[h, t] = bank(PACK * (1 - h) + t)
+        for a in range(PASSES):
+            for h in order:
+                v_w[a, h] = held([P, N], U32, "v_w%d_%d" % (a, h))
+                cols = slice(h * N // 16, (h + 1) * N // 16)
+                nc.vector.tensor_copy(v_w[a, h][:], tab_w[a][:].bitcast(U32).indirect(offs_sb[:, cols]))
+            if a == 0:
+                nc.vector.tensor_copy(v_s[0][:], tab_s[:].indirect(offs_sb[:]))
+                for b in range(1, PASSES):
+                    nc.scalar.dma_start(v_s[b][0:112, :].bitcast(I32), v_s[0][4 * b : 4 * b + 112, :].bitcast(I32))
+            for h in order:
+                for t in range(PACK):
+                    nc.tensor.matmul_mx(
+                        wear_ps[h, t][:],
+                        lhsT=w4_w[:, a, 2 * P * t : 2 * P * (t + 1)].bitcast(FP4X4),
+                        lhsT_scale=w4_s[:, a, P * t : P * (t + 1)],
+                        rhs=v_w[a, h][:].bitcast(FP8X4),
+                        rhs_scale=v_s[a][:, h * N : (h + 1) * N],
+                        start=(a == 0), stop=(a == PASSES - 1),
+                    )
+
+        w1_rows = w1.rearrange("(a p j) c -> a p j c", p=P, j=PACK)
+        HC = H // 2
+        w1_raw = {}
+        first = streamed([P, (PASSES - 1) * PACK * H], F32)
+        for a in range(PASSES - 1):
+            whole = first[:, a * PACK * H : (a + 1) * PACK * H].rearrange("p (j c) -> p j c", j=PACK)
+            nc.sync.dma_start(whole, w1_rows[a])
+            for c in range(2):
+                w1_raw[a, c] = whole[:, :, c * HC : (c + 1) * HC]
+        last = streamed([P, PACK * H], F32)
+        for c in range(2):
+            part = last[:, c * PACK * HC : (c + 1) * PACK * HC].rearrange("p (j c) -> p j c", j=PACK)
+            nc.sync.dma_start(part, w1_rows[PASSES - 1][:, :, c * HC : (c + 1) * HC])
+            w1_raw[PASSES - 1, c] = part
+
+        v2_s = held([P, S2], U8, "v2_s")
+        for g in range(M_TILES // 2):
+            nc.vector.tensor_copy(v2_s[:, 2 * P * g : 2 * P * (g + 1)], tab2_s[:].indirect(offs2_sb[:, 16 * g : 16 * (g + 1)]))
+
+        wear = {}
+        for t in range(PACK):
+            wear[0, t] = wear_ps[0, t]
+            wear[1, t] = held([P, N], F32, "wear_sb%d" % t)
+            nc.scalar.copy(wear[1, t][:], wear_ps[1, t][:])
+
+        w1_w = [held([P, H], U32, "w1_w%d" % a) for a in range(PASSES)]
+        w1_s = [held([P, H], U8, "w1_s%d" % a) for a in range(PASSES)]
+
+        def tread_pass(acc, a, h, t):
+            nc.tensor.matmul_mx(
+                acc[:],
+                lhsT=w1_w[a][:, P * t : P * (t + 1)].bitcast(FP8X4),
+                lhsT_scale=w1_s[a][:, P * t : P * (t + 1)],
+                rhs=v_w[a, h][:].bitcast(FP8X4),
+                rhs_scale=v_s[a][:, h * N : (h + 1) * N],
+                start=(a == 0), stop=(a == PASSES - 1),
+            )
+
+        tread = {}
+        for t in range(PACK):
+            tread[0, t] = bank(t)
+        on_scalar = [(1, 1), (2, 0)]
+        for a in range(PASSES):
+            w1_bf = held([P, PACK, P, PACK], BF16, "w1_bf%d" % a)
+            for c in range(2):
+                dst = w1_bf[:, :, c * P // 2 : (c + 1) * P // 2, :].rearrange("p t m j -> p m t j")
+                src = w1_raw[a, c].rearrange("p j (m t) -> p m t j", t=PACK)
+                if (a, c) in on_scalar:
+                    nc.scalar.copy(dst, src)
+                else:
+                    nc.vector.tensor_copy(dst, src)
+            for t in range(PACK):
+                nc.vector.quantize_mx(
+                    w1_w[a][:, P * t : P * (t + 1)].bitcast(FP8X4),
+                    w1_s[a][:, P * t : P * (t + 1)],
+                    w1_bf[:, t, :, :].rearrange("p m j -> p (m j)"),
+                )
+                tread_pass(tread[0, t], a, 0, t)
+
+        tab2_w = streamed([P, T2], I32)
+        nc.sync.dma_start(tab2_w[:], tab2_words[0].rearrange("p t i -> p (t i)").bitcast(I32))
+        base_sb = held([P, M_TILES], F32, "w1_bf%d" % (PASSES - 1))
+        with nc.allow_non_contiguous_dma(reason="one base value for each output row"):
+            nc.sync.dma_start(base_sb[:], base.rearrange("(i p) -> p i", p=P))
+        h_w = [held([P, N], U32, "h_w%d" % h) for h in range(HALVES)]
+        h_s = [held([P, N], U8, "h_s%d" % h) for h in range(HALVES)]
+        v2_w = [held([P, 2 * P], U32, "v2_w%d" % g) for g in range(M_TILES // 2)]
+
+        def gather_v2(g):
+            nc.vector.tensor_copy(v2_w[g][:], tab2_w[:].bitcast(U32).indirect(offs2_sb[:, 16 * g : 16 * (g + 1)]))
+
+        for h in range(HALVES):
+            h_rows = held([P, PACK, N], BF16, "h_rows%d" % h)
+            bounded = {}
+            for t in range(PACK):
+                if h == 1:
+                    tread[1, t] = bank(t)
+                    for a in range(PASSES):
+                        tread_pass(tread[1, t], a, 1, t)
+                bounded[t] = ring.tile([P, N], F32, name="bounded")
+                nc.scalar.activation(bounded[t][:], tread[h, t][:], ACT.Tanh, bias=b1_sb[:, t : t + 1])
+            for t in range(PACK):
+                larger = ring.tile([P, N], F32, name="larger")
+                nc.vector.tensor_tensor(larger[:], wear[h, t][:], bounded[t][:], ALU.max)
+                nc.scalar.activation(h_rows[:, t, :], larger[:], ACT.Copy, scale=gain_sb[:, t : t + 1])
+            h_bf = held([P, N, PACK], BF16, "h_bf%d" % h)
+            nc.vector.tensor_copy(
+                h_bf[:].rearrange("p (c i) t -> p c t i", i=4),
+                h_rows[:].rearrange("p t (c i) -> p c t i", i=4),
+            )
+            gather_v2(h)
+            nc.vector.quantize_mx(h_w[h][:].bitcast(FP8X4), h_s[h][:], h_bf[:].rearrange("p j t -> p (j t)"))
+        for g in range(HALVES, M_TILES // 2):
+            gather_v2(g)
+
+        scores, toes, diffs = {}, {}, {}
+
+        def score(i):
+            scores[i] = ring.tile([P, S], F32, name="scores")
+            for h in range(HALVES):
+                acc = bank((PACK + HALVES * i + h) % 8)
+                nc.tensor.matmul_mx(
+                    acc[:],
+                    lhsT=v2_w[i // 2][:, P * (i % 2) : P * (i % 2 + 1)].bitcast(FP8X4),
+                    lhsT_scale=v2_s[:, P * i : P * (i + 1)],
+                    rhs=h_w[h][:].bitcast(FP8X4),
+                    rhs_scale=h_s[h][:],
+                    start=True, stop=True,
+                )
+                nc.scalar.copy(scores[i][:, h * N : (h + 1) * N], acc[:])
+
+        def pick_toe(i):
+            toes[i] = ring.tile([P, PAIRS], F32, name="toes")
+            nc.vector.tensor_copy(toes[i][:], scores[i][:].indirect(pos2_sb[:]))
+
+        def subtract(i):
+            diffs[i] = ring.tile([P, PAIRS], F32, name="diffs")
+            nc.vector.tensor_tensor(diffs[i][:], scores[i][:].indirect(pos1_sb[:]), toes[i][:], ALU.subtract)
+
+        def finish(i):
+            result = ring.tile([P, PAIRS], F32, name="result")
+            nc.vector.tensor_scalar(result[:], diffs[i][:], base_sb[:, i : i + 1], None, ALU.max)
+            nc.sync.dma_start(out[P * i : P * (i + 1), :], result[:])
+
+        for step in range(M_TILES + 2):
+            if step < M_TILES:
+                score(step)
+                pick_toe(step)
+            if 1 <= step <= M_TILES:
+                subtract(step - 1)
+            if step >= 2:
+                finish(step - 2)

@@ -33,7 +33,6 @@ def tile_list_sole_link_scores_kernel(
     with ExitStack() as ctx:
         keep = ctx.enter_context(tc.tile_pool(name="keep", bufs=1))
         ring = ctx.enter_context(tc.tile_pool(name="ring", bufs=4))
-        stream = ctx.enter_context(tc.tile_pool(name="stream", bufs=3))
         psum = ctx.enter_context(tc.psum_pool(name="psum", bufs=1))
 
         def held(shape, dtype, name):
@@ -47,11 +46,11 @@ def tile_list_sole_link_scores_kernel(
         pos1_sb = held([P, PAIRS // 16], U16, "pos1_sb")
         pos2_sb = held([P, PAIRS // 16], U16, "pos2_sb")
 
-        def streamed(shape, dtype):
-            return stream.tile(shape, dtype, name="streamed", align_bytes=64)
-
+        tab_w = [held([P, T], I32, "tab_w%d" % a) for a in range(PASSES)]
         tab_s = held([P, T], U8, "tab_s")
+        tab2_w = held([P, T2], I32, "tab2_w")
         tab2_s = held([P, T2], U8, "tab2_s")
+        w4_raw = held([P, PASSES, 2 * H], U8, "w4_raw")
         w4s_raw = held([P, PASSES, H], U8, "w4s_raw")
         v_s = [held([P, S], U8, "v_s%d" % a) for a in range(PASSES)]
         warm = held([P, 1], F32, "warm")
@@ -59,43 +58,61 @@ def tile_list_sole_link_scores_kernel(
         b1_sb = held([P, PACK], F32, "b1_sb")
         gain_sb = held([P, PACK], F32, "gain_sb")
 
-        nc.vector.memset(tab_s[:].bitcast(I32), 0)
         nc.vector.memset(w4s_raw[:].rearrange("p a c -> p (a c)").bitcast(I32), 0)
+        nc.vector.memset(tab_s[:].bitcast(I32), 0)
         nc.vector.memset(tab2_s[:].bitcast(I32), 0)
         for a in range(1, PASSES):
             nc.vector.memset(v_s[a][:].bitcast(I32), 0)
         nc.vector.memset(warm[:], 0.0)
 
         def load_table(a):
-            words = streamed([P, T], I32)
-            nc.sync.dma_start(words[:], tab_words[a].rearrange("p t i -> p (t i)").bitcast(I32))
-            return words
+            nc.sync.dma_start(tab_w[a][:], tab_words[a].rearrange("p t i -> p (t i)").bitcast(I32))
+
+        w1_rows = w1.rearrange("(a p j) c -> a p j c", p=P, j=PACK)
+        HC = H // 2
+        w1_raw = {}
+
+        def load_w1(a, parts):
+            width = H // parts
+            for part in range(parts):
+                raw = held([P, PACK, width], F32, "w1_raw%d_%d" % (a, part))
+                nc.sync.dma_start(raw[:], w1_rows[a][:, :, part * width : (part + 1) * width])
+                for c in range(width // HC):
+                    w1_raw[a, part + c] = raw[:, :, c * HC : (c + 1) * HC]
 
         nc.sync.dma_start(offs_sb[:], offs)
-        nc.sync.dma_start(offs2_sb[:], offs2)
-        nc.sync.dma_start(b1_sb[:], b1.rearrange("(p t) -> p t", t=PACK))
-        nc.sync.dma_start(gain_sb[:], gain.rearrange("(p t) -> p t", t=PACK))
-        w4_raw = streamed([P, PASSES, 2 * H], U8)
         nc.sync.dma_start(w4_raw[:].bitcast(I32), w4_words.rearrange("a p c -> p a c").bitcast(I32))
-        tab_w = [load_table(0), load_table(1)]
-        nc.sync.dma_start(pos1_sb[:], pos1)
-        nc.sync.dma_start(pos2_sb[:], pos2)
         for q in range(QUADS):
-            nc.gpsimd.dma_start(
-                tab_s[32 * q : 32 * q + 4 * PASSES, :].bitcast(I32),
-                tab_scales[:, 4 * q : 4 * q + 4, :].bitcast(I32),
-            )
-        for q in range(QUADS):
-            nc.scalar.dma_start(
+            nc.sync.dma_start(
                 w4s_raw[32 * q : 32 * q + 4, :, :].bitcast(I32),
                 w4_scales[:, 4 * q : 4 * q + 4, :].rearrange("a r c -> r a c").bitcast(I32),
             )
+        load_table(0)
         for q in range(QUADS):
-            nc.gpsimd.dma_start(
+            nc.scalar.dma_start(
+                tab_s[32 * q : 32 * q + 4 * PASSES, :].bitcast(I32),
+                tab_scales[:, 4 * q : 4 * q + 4, :].bitcast(I32),
+            )
+        nc.scalar.activation(warm_out[:], warm[:], ACT.Tanh)
+        load_w1(0, 1)
+        nc.sync.dma_start(offs2_sb[:], offs2)
+        load_table(1)
+        for q in range(QUADS):
+            nc.sync.dma_start(
                 tab2_s[32 * q : 32 * q + 4, :].bitcast(I32),
                 tab2_scales[0, 4 * q : 4 * q + 4, :].bitcast(I32),
             )
-        nc.scalar.activation(warm_out[:], warm[:], ACT.Tanh)
+        load_w1(1, 1)
+        load_table(2)
+        nc.sync.dma_start(b1_sb[:], b1.rearrange("(p t) -> p t", t=PACK))
+        nc.sync.dma_start(gain_sb[:], gain.rearrange("(p t) -> p t", t=PACK))
+        load_w1(2, 2)
+        nc.sync.dma_start(tab2_w[:], tab2_words[0].rearrange("p t i -> p (t i)").bitcast(I32))
+        nc.sync.dma_start(pos1_sb[:], pos1)
+        nc.sync.dma_start(pos2_sb[:], pos2)
+        base_sb = held([P, M_TILES], F32, "base_sb")
+        with nc.allow_non_contiguous_dma(reason="one base value for each output row"):
+            nc.sync.dma_start(base_sb[:], base.rearrange("(i p) -> p i", p=P))
 
         w4_w = held([P, PASSES, 2 * H], U8, "w4_w")
         w4_s = held([P, PASSES, H], U8, "w4_s")
@@ -108,7 +125,6 @@ def tile_list_sole_link_scores_kernel(
             w4s_raw[:].rearrange("p a (m t) -> p a m t", t=PACK),
         )
 
-        tab_w.append(load_table(2))
         v_w = {}
         wear_ps = {}
         order = list(reversed(range(HALVES)))
@@ -134,21 +150,6 @@ def tile_list_sole_link_scores_kernel(
                         rhs_scale=v_s[a][:, h * N : (h + 1) * N],
                         start=(a == 0), stop=(a == PASSES - 1),
                     )
-
-        w1_rows = w1.rearrange("(a p j) c -> a p j c", p=P, j=PACK)
-        HC = H // 2
-        w1_raw = {}
-        first = streamed([P, (PASSES - 1) * PACK * H], F32)
-        for a in range(PASSES - 1):
-            whole = first[:, a * PACK * H : (a + 1) * PACK * H].rearrange("p (j c) -> p j c", j=PACK)
-            nc.sync.dma_start(whole, w1_rows[a])
-            for c in range(2):
-                w1_raw[a, c] = whole[:, :, c * HC : (c + 1) * HC]
-        last = streamed([P, PACK * H], F32)
-        for c in range(2):
-            part = last[:, c * PACK * HC : (c + 1) * PACK * HC].rearrange("p (j c) -> p j c", j=PACK)
-            nc.sync.dma_start(part, w1_rows[PASSES - 1][:, :, c * HC : (c + 1) * HC])
-            w1_raw[PASSES - 1, c] = part
 
         v2_s = held([P, S2], U8, "v2_s")
         for g in range(M_TILES // 2):
@@ -176,7 +177,7 @@ def tile_list_sole_link_scores_kernel(
         tread = {}
         for t in range(PACK):
             tread[0, t] = bank(t)
-        on_scalar = [(1, 1), (2, 0)]
+        on_scalar = [(0, 0), (0, 1), (1, 0), (1, 1)]
         for a in range(PASSES):
             w1_bf = held([P, PACK, P, PACK], BF16, "w1_bf%d" % a)
             for c in range(2):
@@ -194,47 +195,53 @@ def tile_list_sole_link_scores_kernel(
                 )
                 tread_pass(tread[0, t], a, 0, t)
 
-        tab2_w = streamed([P, T2], I32)
-        nc.sync.dma_start(tab2_w[:], tab2_words[0].rearrange("p t i -> p (t i)").bitcast(I32))
-        base_sb = held([P, M_TILES], F32, "w1_bf%d" % (PASSES - 1))
-        with nc.allow_non_contiguous_dma(reason="one base value for each output row"):
-            nc.sync.dma_start(base_sb[:], base.rearrange("(i p) -> p i", p=P))
         h_w = [held([P, N], U32, "h_w%d" % h) for h in range(HALVES)]
         h_s = [held([P, N], U8, "h_s%d" % h) for h in range(HALVES)]
         v2_w = [held([P, 2 * P], U32, "v2_w%d" % g) for g in range(M_TILES // 2)]
 
-        def gather_v2(g):
+
+        def gather_soles(g):
             nc.vector.tensor_copy(v2_w[g][:], tab2_w[:].bitcast(U32).indirect(offs2_sb[:, 16 * g : 16 * (g + 1)]))
 
-        for h in range(HALVES):
-            h_rows = held([P, PACK, N], BF16, "h_rows%d" % h)
-            bounded = {}
-            for t in range(PACK):
-                if h == 1:
-                    tread[1, t] = bank(t)
-                    for a in range(PASSES):
-                        tread_pass(tread[1, t], a, 1, t)
-                bounded[t] = ring.tile([P, N], F32, name="bounded")
-                nc.scalar.activation(bounded[t][:], tread[h, t][:], ACT.Tanh, bias=b1_sb[:, t : t + 1])
-            for t in range(PACK):
-                larger = ring.tile([P, N], F32, name="larger")
-                nc.vector.tensor_tensor(larger[:], wear[h, t][:], bounded[t][:], ALU.max)
-                nc.scalar.activation(h_rows[:, t, :], larger[:], ACT.Copy, scale=gain_sb[:, t : t + 1])
-            h_bf = held([P, N, PACK], BF16, "h_bf%d" % h)
-            nc.vector.tensor_copy(
-                h_bf[:].rearrange("p (c i) t -> p c t i", i=4),
-                h_rows[:].rearrange("p t (c i) -> p c t i", i=4),
-            )
-            gather_v2(h)
-            nc.vector.quantize_mx(h_w[h][:].bitcast(FP8X4), h_s[h][:], h_bf[:].rearrange("p j t -> p (j t)"))
-        for g in range(HALVES, M_TILES // 2):
-            gather_v2(g)
+        larger = {}
+        h_rows = [held([P, PACK, N], BF16, "h_rows%d" % h) for h in range(HALVES)]
+        h_bf = [held([P, N, PACK], BF16, "h_bf%d" % h) for h in range(HALVES)]
+
+        def compare(h, t):
+            bounded = ring.tile([P, N], F32, name="bounded")
+            nc.scalar.activation(bounded[:], tread[h, t][:], ACT.Tanh, bias=b1_sb[:, t : t + 1])
+            larger[h, t] = held([P, N], F32, "larger%d_%d" % (h, t))
+            nc.vector.tensor_tensor(larger[h, t][:], wear[h, t][:], bounded[:], ALU.max)
+
+        def weave(copy, h):
+            copy(h_bf[h][:].rearrange("p (c i) t -> p c t i", i=4), h_rows[h][:].rearrange("p t (c i) -> p c t i", i=4))
+
+        def quantise_h(h):
+            nc.vector.quantize_mx(h_w[h][:].bitcast(FP8X4), h_s[h][:], h_bf[h][:].rearrange("p j t -> p (j t)"))
+
+        for t in range(PACK):
+            compare(0, t)
+        gather_soles(0)
+        for t in range(PACK):
+            tread[1, t] = bank(t)
+            for a in range(PASSES):
+                tread_pass(tread[1, t], a, 1, t)
+            compare(1, t)
+            nc.scalar.activation(h_rows[0][:, t, :], larger[0, t][:], ACT.Copy, scale=gain_sb[:, t : t + 1])
+        weave(nc.scalar.copy, 0)
+        for t in range(PACK):
+            nc.vector.tensor_scalar(h_rows[1][:, t, :], larger[1, t][:], gain_sb[:, t : t + 1], None, ALU.mult)
+        weave(nc.vector.tensor_copy, 1)
+        quantise_h(1)
+        quantise_h(0)
+        for g in range(1, M_TILES // 2):
+            gather_soles(g)
 
         scores, toes, diffs = {}, {}, {}
 
         def score(i):
             scores[i] = ring.tile([P, S], F32, name="scores")
-            for h in range(HALVES):
+            for h in order:
                 acc = bank((PACK + HALVES * i + h) % 8)
                 nc.tensor.matmul_mx(
                     acc[:],

@@ -58,12 +58,13 @@ def tile_list_sole_link_scores_kernel(
         b1_sb = held([P, PACK], F32, "b1_sb")
         gain_sb = held([P, PACK], F32, "gain_sb")
 
-        nc.vector.memset(w4s_raw[:].rearrange("p a c -> p (a c)").bitcast(I32), 0)
+        nc.gpsimd.memset(tab2_s[:].bitcast(I32), 0)
         nc.vector.memset(tab_s[:].bitcast(I32), 0)
-        nc.vector.memset(tab2_s[:].bitcast(I32), 0)
+        nc.vector.memset(w4s_raw[:].rearrange("p a c -> p (a c)").bitcast(I32), 0)
         for a in range(1, PASSES):
             nc.vector.memset(v_s[a][:].bitcast(I32), 0)
         nc.vector.memset(warm[:], 0.0)
+        nc.scalar.activation(warm_out[:], warm[:], ACT.Tanh)
 
         def load_table(a):
             nc.sync.dma_start(tab_w[a][:], tab_words[a].rearrange("p t i -> p (t i)").bitcast(I32))
@@ -80,28 +81,27 @@ def tile_list_sole_link_scores_kernel(
                 for c in range(width // HC):
                     w1_raw[a, part + c] = raw[:, :, c * HC : (c + 1) * HC]
 
-        nc.sync.dma_start(offs_sb[:], offs)
-        nc.sync.dma_start(w4_raw[:].bitcast(I32), w4_words.rearrange("a p c -> p a c").bitcast(I32))
-        for q in range(QUADS):
-            nc.sync.dma_start(
-                w4s_raw[32 * q : 32 * q + 4, :, :].bitcast(I32),
-                w4_scales[:, 4 * q : 4 * q + 4, :].rearrange("a r c -> r a c").bitcast(I32),
-            )
-        load_table(0)
-        for q in range(QUADS):
-            nc.scalar.dma_start(
-                tab_s[32 * q : 32 * q + 4 * PASSES, :].bitcast(I32),
-                tab_scales[:, 4 * q : 4 * q + 4, :].bitcast(I32),
-            )
-        nc.scalar.activation(warm_out[:], warm[:], ACT.Tanh)
-        load_w1(0, 1)
         nc.sync.dma_start(offs2_sb[:], offs2)
-        load_table(1)
+        nc.sync.dma_start(offs_sb[:], offs)
         for q in range(QUADS):
             nc.sync.dma_start(
                 tab2_s[32 * q : 32 * q + 4, :].bitcast(I32),
                 tab2_scales[0, 4 * q : 4 * q + 4, :].bitcast(I32),
             )
+        load_table(0)
+        nc.sync.dma_start(w4_raw[:].bitcast(I32), w4_words.rearrange("a p c -> p a c").bitcast(I32))
+        for q in range(QUADS):
+            nc.sync.dma_start(
+                tab_s[32 * q : 32 * q + 4 * PASSES, :].bitcast(I32),
+                tab_scales[:, 4 * q : 4 * q + 4, :].bitcast(I32),
+            )
+        load_w1(0, 1)
+        for q in range(QUADS):
+            nc.sync.dma_start(
+                w4s_raw[32 * q : 32 * q + 4, :, :].bitcast(I32),
+                w4_scales[:, 4 * q : 4 * q + 4, :].rearrange("a r c -> r a c").bitcast(I32),
+            )
+        load_table(1)
         load_w1(1, 1)
         load_table(2)
         nc.sync.dma_start(b1_sb[:], b1.rearrange("(p t) -> p t", t=PACK))
@@ -117,12 +117,12 @@ def tile_list_sole_link_scores_kernel(
         w4_w = held([P, PASSES, 2 * H], U8, "w4_w")
         w4_s = held([P, PASSES, H], U8, "w4_s")
         nc.vector.tensor_copy(
-            w4_w[:].bitcast(U16).rearrange("p a (t m) -> p a m t", t=PACK),
-            w4_raw[:].bitcast(U16).rearrange("p a (m t) -> p a m t", t=PACK),
+            w4_w[:].bitcast(U16).rearrange("p a (t u m) -> p u a m t", t=PACK, u=2),
+            w4_raw[:].bitcast(U16).rearrange("p a (u m t) -> p u a m t", t=PACK, u=2),
         )
         nc.vector.tensor_copy(
-            w4_s[:].rearrange("p a (t m) -> p a m t", t=PACK),
-            w4s_raw[:].rearrange("p a (m t) -> p a m t", t=PACK),
+            w4_s[:].rearrange("p a (t u m) -> p u a m t", t=PACK, u=2),
+            w4s_raw[:].rearrange("p a (u m t) -> p u a m t", t=PACK, u=2),
         )
 
         v_w = {}
@@ -152,8 +152,7 @@ def tile_list_sole_link_scores_kernel(
                     )
 
         v2_s = held([P, S2], U8, "v2_s")
-        for g in range(M_TILES // 2):
-            nc.vector.tensor_copy(v2_s[:, 2 * P * g : 2 * P * (g + 1)], tab2_s[:].indirect(offs2_sb[:, 16 * g : 16 * (g + 1)]))
+        nc.vector.tensor_copy(v2_s[:], tab2_s[:].indirect(offs2_sb[:]))
 
         wear = {}
         for t in range(PACK):
@@ -197,11 +196,12 @@ def tile_list_sole_link_scores_kernel(
 
         h_w = [held([P, N], U32, "h_w%d" % h) for h in range(HALVES)]
         h_s = [held([P, N], U8, "h_s%d" % h) for h in range(HALVES)]
-        v2_w = [held([P, 2 * P], U32, "v2_w%d" % g) for g in range(M_TILES // 2)]
+        v2_w = {}
 
 
-        def gather_soles(g):
-            nc.vector.tensor_copy(v2_w[g][:], tab2_w[:].bitcast(U32).indirect(offs2_sb[:, 16 * g : 16 * (g + 1)]))
+        def gather_soles(g, slot):
+            v2_w[g] = held([P, S2 // 2], U32, slot)
+            nc.vector.tensor_copy(v2_w[g][:], tab2_w[:].bitcast(U32).indirect(offs2_sb[:, 32 * g : 32 * (g + 1)]))
 
         larger = {}
         h_rows = [held([P, PACK, N], BF16, "h_rows%d" % h) for h in range(HALVES)]
@@ -213,6 +213,9 @@ def tile_list_sole_link_scores_kernel(
             larger[h, t] = held([P, N], F32, "larger%d_%d" % (h, t))
             nc.vector.tensor_tensor(larger[h, t][:], wear[h, t][:], bounded[:], ALU.max)
 
+        def scale_on_scalar(t):
+            nc.scalar.activation(h_rows[0][:, t, :], larger[0, t][:], ACT.Copy, scale=gain_sb[:, t : t + 1])
+
         def weave(copy, h):
             copy(h_bf[h][:].rearrange("p (c i) t -> p c t i", i=4), h_rows[h][:].rearrange("p t (c i) -> p c t i", i=4))
 
@@ -221,21 +224,22 @@ def tile_list_sole_link_scores_kernel(
 
         for t in range(PACK):
             compare(0, t)
-        gather_soles(0)
+        gather_soles(0, "v2_w0")
         for t in range(PACK):
             tread[1, t] = bank(t)
             for a in range(PASSES):
                 tread_pass(tread[1, t], a, 1, t)
             compare(1, t)
-            nc.scalar.activation(h_rows[0][:, t, :], larger[0, t][:], ACT.Copy, scale=gain_sb[:, t : t + 1])
-        weave(nc.scalar.copy, 0)
-        for t in range(PACK):
+            if t % 2 == 0:
+                scale_on_scalar(t // 2)
             nc.vector.tensor_scalar(h_rows[1][:, t, :], larger[1, t][:], gain_sb[:, t : t + 1], None, ALU.mult)
+        for t in range(PACK // 2, PACK):
+            scale_on_scalar(t)
+        weave(nc.scalar.copy, 0)
         weave(nc.vector.tensor_copy, 1)
         quantise_h(1)
         quantise_h(0)
-        for g in range(1, M_TILES // 2):
-            gather_soles(g)
+        gather_soles(1, "h_bf0")
 
         scores, toes, diffs = {}, {}, {}
 
@@ -245,7 +249,7 @@ def tile_list_sole_link_scores_kernel(
                 acc = bank((PACK + HALVES * i + h) % 8)
                 nc.tensor.matmul_mx(
                     acc[:],
-                    lhsT=v2_w[i // 2][:, P * (i % 2) : P * (i % 2 + 1)].bitcast(FP8X4),
+                    lhsT=v2_w[i // 4][:, P * (i % 4) : P * (i % 4 + 1)].bitcast(FP8X4),
                     lhsT_scale=v2_s[:, P * i : P * (i + 1)],
                     rhs=h_w[h][:].bitcast(FP8X4),
                     rhs_scale=h_s[h][:],

from contextlib import ExitStack

import concourse.mybir as mybir

K, H, T, S, T2, S2, PAIRS = 1536, 512, 4096, 1024, 2048, 1024, 512
FLOPS = 2 * K * H * S * 2 + 2 * H * S2 * S

F32 = mybir.dt.float32
BF16 = mybir.dt.bfloat16
I32 = mybir.dt.int32
U32 = mybir.dt.uint32
U16 = mybir.dt.uint16
U8 = mybir.dt.uint8
FP8X4 = mybir.dt.float8_e4m3fn_x4
FP4X4 = mybir.dt.float4_e2m1fn_x4
ACT = mybir.ActivationFunctionType
ALU = mybir.AluOpType

P = 128
PACK = 4
PASSES = K // (P * PACK)
N = 512
HALVES = S // N
QUADS = 4
M_TILES = S2 // P


def tile_list_sole_link_scores_kernel(
    tc, tab_words, tab_scales, offs, tab2_words, tab2_scales, offs2, pos1, pos2,
    w1, b1, w4_words, w4_scales, gain, base, out,
):
    nc = tc.nc
    with ExitStack() as ctx:
        keep = ctx.enter_context(tc.tile_pool(name="keep", bufs=1))
        ring = ctx.enter_context(tc.tile_pool(name="ring", bufs=4))
        psum = ctx.enter_context(tc.psum_pool(name="psum", bufs=1))

        def held(shape, dtype, name):
            return keep.tile(shape, dtype, name=name, align_bytes=64)

        def bank(b):
            return psum.tile([P, N], F32, name="bank%d" % b)

        offs_sb = held([P, S // 16], U16, "offs_sb")
        offs2_sb = held([P, S2 // 16], U16, "offs2_sb")
        pos1_sb = held([P, PAIRS // 16], U16, "pos1_sb")
        pos2_sb = held([P, PAIRS // 16], U16, "pos2_sb")

        tab_w = [held([P, T], I32, "tab_w%d" % a) for a in range(PASSES)]
        tab_s = held([P, T], U8, "tab_s")
        tab2_w = held([P, T2], I32, "tab2_w")
        tab2_s = held([P, T2], U8, "tab2_s")
        w4_raw = held([P, PASSES, 2 * H], U8, "w4_raw")
        w4s_raw = held([P, PASSES, H], U8, "w4s_raw")
        v_s = [held([P, S], U8, "v_s%d" % a) for a in range(PASSES)]
        warm = held([P, 1], F32, "warm")
        warm_out = held([P, 1], F32, "warm_out")
        b1_sb = held([P, PACK], F32, "b1_sb")
        gain_sb = held([P, PACK], F32, "gain_sb")

        nc.gpsimd.memset(tab2_s[:].bitcast(I32), 0)
        nc.vector.memset(tab_s[:].bitcast(I32), 0)
        nc.vector.memset(w4s_raw[:].rearrange("p a c -> p (a c)").bitcast(I32), 0)
        for a in range(1, PASSES):
            nc.vector.memset(v_s[a][:].bitcast(I32), 0)
        nc.vector.memset(warm[:], 0.0)
        nc.scalar.activation(warm_out[:], warm[:], ACT.Tanh)

        def load_table(a):
            nc.sync.dma_start(tab_w[a][:], tab_words[a].rearrange("p t i -> p (t i)").bitcast(I32))

        w1_rows = w1.rearrange("(a p j) c -> a p j c", p=P, j=PACK)
        HC = H // 2
        w1_raw = {}

        def load_w1(a, parts):
            width = H // parts
            for part in range(parts):
                raw = held([P, PACK, width], F32, "w1_raw%d_%d" % (a, part))
                nc.sync.dma_start(raw[:], w1_rows[a][:, :, part * width : (part + 1) * width])
                for c in range(width // HC):
                    w1_raw[a, part + c] = raw[:, :, c * HC : (c + 1) * HC]

        nc.sync.dma_start(offs2_sb[:], offs2)
        nc.sync.dma_start(offs_sb[:], offs)
        for q in range(QUADS):
            nc.sync.dma_start(
                tab2_s[32 * q : 32 * q + 4, :].bitcast(I32),
                tab2_scales[0, 4 * q : 4 * q + 4, :].bitcast(I32),
            )
        load_table(0)
        nc.sync.dma_start(w4_raw[:].bitcast(I32), w4_words.rearrange("a p c -> p a c").bitcast(I32))
        for q in range(QUADS):
            nc.sync.dma_start(
                tab_s[32 * q : 32 * q + 4 * PASSES, :].bitcast(I32),
                tab_scales[:, 4 * q : 4 * q + 4, :].bitcast(I32),
            )
        load_w1(0, 1)
        for q in range(QUADS):
            nc.sync.dma_start(
                w4s_raw[32 * q : 32 * q + 4, :, :].bitcast(I32),
                w4_scales[:, 4 * q : 4 * q + 4, :].rearrange("a r c -> r a c").bitcast(I32),
            )
        load_table(1)
        load_w1(1, 1)
        load_table(2)
        nc.sync.dma_start(b1_sb[:], b1.rearrange("(p t) -> p t", t=PACK))
        nc.sync.dma_start(gain_sb[:], gain.rearrange("(p t) -> p t", t=PACK))
        load_w1(2, 2)
        nc.sync.dma_start(tab2_w[:], tab2_words[0].rearrange("p t i -> p (t i)").bitcast(I32))
        nc.sync.dma_start(pos1_sb[:], pos1)
        nc.sync.dma_start(pos2_sb[:], pos2)
        base_sb = held([P, M_TILES], F32, "base_sb")
        with nc.allow_non_contiguous_dma(reason="one base value for each output row"):
            nc.sync.dma_start(base_sb[:], base.rearrange("(i p) -> p i", p=P))

        w4_w = held([P, PASSES, 2 * H], U8, "w4_w")
        w4_s = held([P, PASSES, H], U8, "w4_s")
        nc.vector.tensor_copy(
            w4_w[:].bitcast(U16).rearrange("p a (t u m) -> p u a m t", t=PACK, u=2),
            w4_raw[:].bitcast(U16).rearrange("p a (u m t) -> p u a m t", t=PACK, u=2),
        )
        nc.vector.tensor_copy(
            w4_s[:].rearrange("p a (t u m) -> p u a m t", t=PACK, u=2),
            w4s_raw[:].rearrange("p a (u m t) -> p u a m t", t=PACK, u=2),
        )

        v_w = {}
        wear_ps = {}
        order = list(reversed(range(HALVES)))
        for h in order:
            for t in range(PACK):
                wear_ps[h, t] = bank(PACK * (1 - h) + t)
        for a in range(PASSES):
            for h in order:
                v_w[a, h] = held([P, N], U32, "v_w%d_%d" % (a, h))
                cols = slice(h * N // 16, (h + 1) * N // 16)
                nc.vector.tensor_copy(v_w[a, h][:], tab_w[a][:].bitcast(U32).indirect(offs_sb[:, cols]))
            if a == 0:
                nc.vector.tensor_copy(v_s[0][:], tab_s[:].indirect(offs_sb[:]))
                for b in range(1, PASSES):
                    nc.scalar.dma_start(v_s[b][0:112, :].bitcast(I32), v_s[0][4 * b : 4 * b + 112, :].bitcast(I32))
            for h in order:
                for t in range(PACK):
                    nc.tensor.matmul_mx(
                        wear_ps[h, t][:],
                        lhsT=w4_w[:, a, 2 * P * t : 2 * P * (t + 1)].bitcast(FP4X4),
                        lhsT_scale=w4_s[:, a, P * t : P * (t + 1)],
                        rhs=v_w[a, h][:].bitcast(FP8X4),
                        rhs_scale=v_s[a][:, h * N : (h + 1) * N],
                        start=(a == 0), stop=(a == PASSES - 1),
                    )

        v2_s = held([P, S2], U8, "v2_s")
        nc.vector.tensor_copy(v2_s[:], tab2_s[:].indirect(offs2_sb[:]))

        wear = {}
        for t in range(PACK):
            wear[0, t] = wear_ps[0, t]
            wear[1, t] = held([P, N], F32, "wear_sb%d" % t)
            nc.scalar.copy(wear[1, t][:], wear_ps[1, t][:])

        w1_w = [held([P, H], U32, "w1_w%d" % a) for a in range(PASSES)]
        w1_s = [held([P, H], U8, "w1_s%d" % a) for a in range(PASSES)]

        def tread_pass(acc, a, h, t):
            nc.tensor.matmul_mx(
                acc[:],
                lhsT=w1_w[a][:, P * t : P * (t + 1)].bitcast(FP8X4),
                lhsT_scale=w1_s[a][:, P * t : P * (t + 1)],
                rhs=v_w[a, h][:].bitcast(FP8X4),
                rhs_scale=v_s[a][:, h * N : (h + 1) * N],
                start=(a == 0), stop=(a == PASSES - 1),
            )

        tread = {}
        for t in range(PACK):
            tread[0, t] = bank(t)
        on_scalar = [(0, 0), (0, 1), (1, 0), (1, 1)]
        for a in range(PASSES):
            w1_bf = held([P, PACK, P, PACK], BF16, "w1_bf%d" % a)
            for c in range(2):
                dst = w1_bf[:, :, c * P // 2 : (c + 1) * P // 2, :].rearrange("p t m j -> p m t j")
                src = w1_raw[a, c].rearrange("p j (m t) -> p m t j", t=PACK)
                if (a, c) in on_scalar:
                    nc.scalar.copy(dst, src)
                else:
                    nc.vector.tensor_copy(dst, src)
            for t in range(PACK):
                nc.vector.quantize_mx(
                    w1_w[a][:, P * t : P * (t + 1)].bitcast(FP8X4),
                    w1_s[a][:, P * t : P * (t + 1)],
                    w1_bf[:, t, :, :].rearrange("p m j -> p (m j)"),
                )
                tread_pass(tread[0, t], a, 0, t)

        h_w = [held([P, N], U32, "h_w%d" % h) for h in range(HALVES)]
        h_s = [held([P, N], U8, "h_s%d" % h) for h in range(HALVES)]
        v2_w = {}


        def gather_soles(g, slot):
            v2_w[g] = held([P, S2 // 2], U32, slot)
            nc.vector.tensor_copy(v2_w[g][:], tab2_w[:].bitcast(U32).indirect(offs2_sb[:, 32 * g : 32 * (g + 1)]))

        larger = {}
        h_rows = [held([P, PACK, N], BF16, "h_rows%d" % h) for h in range(HALVES)]
        h_bf = [held([P, N, PACK], BF16, "h_bf%d" % h) for h in range(HALVES)]

        def compare(h, t):
            bounded = ring.tile([P, N], F32, name="bounded")
            nc.scalar.activation(bounded[:], tread[h, t][:], ACT.Tanh, bias=b1_sb[:, t : t + 1])
            larger[h, t] = held([P, N], F32, "larger%d_%d" % (h, t))
            nc.vector.tensor_tensor(larger[h, t][:], wear[h, t][:], bounded[:], ALU.max)

        def scale_on_scalar(t):
            nc.scalar.activation(h_rows[0][:, t, :], larger[0, t][:], ACT.Copy, scale=gain_sb[:, t : t + 1])

        def weave(copy, h):
            copy(h_bf[h][:].rearrange("p (c i) t -> p c t i", i=4), h_rows[h][:].rearrange("p t (c i) -> p c t i", i=4))

        def quantise_h(h):
            nc.vector.quantize_mx(h_w[h][:].bitcast(FP8X4), h_s[h][:], h_bf[h][:].rearrange("p j t -> p (j t)"))

        for t in range(PACK):
            compare(0, t)
        gather_soles(0, "v2_w0")
        for t in range(PACK):
            tread[1, t] = bank(t)
            for a in range(PASSES):
                tread_pass(tread[1, t], a, 1, t)
            compare(1, t)
            if t % 2 == 0:
                scale_on_scalar(t // 2)
            nc.vector.tensor_scalar(h_rows[1][:, t, :], larger[1, t][:], gain_sb[:, t : t + 1], None, ALU.mult)
        for t in range(PACK // 2, PACK):
            scale_on_scalar(t)
        weave(nc.scalar.copy, 0)
        weave(nc.vector.tensor_copy, 1)
        quantise_h(1)
        quantise_h(0)
        gather_soles(1, "h_bf0")

        scores, toes, diffs = {}, {}, {}

        def score(i):
            scores[i] = ring.tile([P, S], F32, name="scores")
            for h in order:
                acc = bank((PACK + HALVES * i + h) % 8)
                nc.tensor.matmul_mx(
                    acc[:],
                    lhsT=v2_w[i // 4][:, P * (i % 4) : P * (i % 4 + 1)].bitcast(FP8X4),
                    lhsT_scale=v2_s[:, P * i : P * (i + 1)],
                    rhs=h_w[h][:].bitcast(FP8X4),
                    rhs_scale=h_s[h][:],
                    start=True, stop=True,
                )
                nc.scalar.copy(scores[i][:, h * N : (h + 1) * N], acc[:])

        def pick_toe(i):
            toes[i] = ring.tile([P, PAIRS], F32, name="toes")
            nc.vector.tensor_copy(toes[i][:], scores[i][:].indirect(pos2_sb[:]))

        def subtract(i):
            diffs[i] = ring.tile([P, PAIRS], F32, name="diffs")
            nc.vector.tensor_tensor(diffs[i][:], scores[i][:].indirect(pos1_sb[:]), toes[i][:], ALU.subtract)

        def finish(i):
            result = ring.tile([P, PAIRS], F32, name="result")
            nc.vector.tensor_scalar(result[:], diffs[i][:], base_sb[:, i : i + 1], None, ALU.max)
            nc.sync.dma_start(out[P * i : P * (i + 1), :], result[:])

        for step in range(M_TILES + 2):
            if step < M_TILES:
                score(step)
                pick_toe(step)
            if 1 <= step <= M_TILES:
                subtract(step - 1)
            if step >= 2:
                finish(step - 2)
